import numpy as np, ml_dtypes
CORES = [40,64,80,88,96,104,120,144]
N = 8
import mx_ref
BF = ml_dtypes.bfloat16
def entries(a):
    return np.ascontiguousarray(a.T).reshape(-1)
def table(e):
    return np.ascontiguousarray(np.reshape(e, (-1, 16)).T).astype(np.int32)
def tile(rs):
    return np.stack(rs, axis=2).reshape(128, -1).astype(BF)
def cut(t, i, w=512):
    return t[:, w * i:w * i + w]
def f(rng, *shape):
    return mx_ref.flush((rng.standard_normal(shape, dtype=np.float32) * np.exp2(rng.integers(-2, 3, shape[:-1] + (1,)))).astype(BF))
def wide(rng, *shape, cols=0):
    v = rng.standard_normal(shape, dtype=np.float32) * np.exp2(rng.integers(-12, 13, shape)).astype(np.float32)
    if cols: v *= np.repeat(np.exp2(rng.integers(-cols, cols + 1, shape[:-2] + (1, shape[-1] // 4))) * (rng.random(shape[:-2] + (1, shape[-1] // 4)) > 0.0625), 4, axis=-1).astype(np.float32)
    return mx_ref.flush(v.astype(BF))
T, TG, C1, C2 = 256, 128, 160, 32
def layer(rng, C, M, own=0.25, full=False, hub=False, neg=None):
    snd = np.full((N, N, C), -1); src = np.zeros((N, M, 4), int)
    for s in range(N):
        for r in range(N):
            if s != r and own < 1:
                n = C if full else rng.integers(1, C + 1)
                snd[s, r, rng.permutation(C)[:n]] = rng.choice(T, n, replace=False)
    h, k, c = rng.integers(0, N), rng.integers(0, T), rng.integers(0, C, N)
    if hub:
        for r in range(N):
            if r != h: snd[h, r, c[r]] = k
    for r in range(N):
        src[r] = rng.integers(0, T, (M, 4))
        if own < 1:
            far = T + np.flatnonzero(snd[:, r].reshape(-1) >= 0)
            src[r] = np.where(rng.random((M, 4)) < own, src[r], rng.choice(far, (M, 4)))
        if hub:
            e = k if r == h else T + h * C + c[r]
            src[r][:, 0] = e; src[r][rng.permutation(M)[:M // 4]] = e
            src[r] = rng.permuted(src[r], axis=1)
        if neg is not None:
            bad = np.flatnonzero(np.concatenate([neg[r]] + [(snd[s, r] >= 0) & neg[s][snd[s, r]] for s in range(N)]))
            src[r][rng.permutation(M)[:M // 2]] = rng.choice(bad, (M // 2, 4))
    return np.stack([table(a) for a in snd]), np.stack([table(a) for a in src])
def lists(rng, neg=None, **o):
    a, b = layer(rng, C1, T, neg=neg, **o); c, e = layer(rng, C2, TG, **o)
    return {"snd1": a, "src1": b, "snd2": c, "src2": e}
def setup_inputs(rng):
    return {"x": f(rng, N, 128, 4 * T), "w1": np.repeat(f(rng, 1, 128, 4 * 512), N, axis=0), "w2": np.repeat(f(rng, 1, 128, 512), N, axis=0), **lists(rng)}
def setup_inputs_foreign(rng):
    return {**setup_inputs(rng), **lists(rng, own=0, full=True)}
def setup_inputs_hub(rng):
    return {**setup_inputs(rng), **lists(rng, hub=True)}
def setup_inputs_negative(rng):
    d = setup_inputs(rng)
    neg = np.stack([rng.permutation(T) < T // 2 for r in range(N)])
    v = np.abs(d["x"]).reshape(N, 128, T, 4)
    d["x"] = np.where(neg[:, None, :, None], -v, v).reshape(N, 128, 4 * T)
    d["w1"] = np.abs(d["w1"])
    return {**d, **lists(rng, neg=neg)}
def setup_inputs_self(rng):
    return {**setup_inputs(rng), **lists(rng, own=1)}
def setup_inputs_spread(rng):
    d = setup_inputs(rng); d["x"] = wide(rng, N, 128, 4 * T); return d
def check_inputs(d):
    b = []
    for k in ("w1", "w2"):
        if any(d[k][r].tobytes() != d[k][0].tobytes() for r in range(N)): b.append(k)
    for l, C in (("1", C1), ("2", C2)):
        snd = np.stack([entries(a) for a in d["snd" + l]]).reshape(N, N, C)
        if snd.min() < -1 or snd.max() >= T: b.append("snd" + l)
        for r in range(N):
            if (snd[r, r] != -1).any(): b.append("snd" + l)
            ok = np.concatenate([np.ones(T, bool), snd[:, r].reshape(-1) >= 0])
            e = entries(d["src" + l][r])
            if e.min() < 0 or e.max() >= T + N * C or not ok[e].all(): b.append("src" + l)
    return b
def most(v, snd, src, r, C):
    a = np.concatenate([v[r]] + [v[s][:, entries(snd[s])[r * C:r * C + C]] for s in range(N)], axis=1)
    return a[:, entries(src[r])].reshape(128, -1, 4).max(axis=2)
def reference(x, w1, w2, snd1, src1, snd2, src2):
    q = [mx_ref.quantize(x[r]) for r in range(N)]
    Z = [[mx_ref.matmul(mx_ref.quantize(cut(w1[r], i)), q[r]) for r in range(N)] for i in range(4)]
    U = []
    for r in range(N):
        h = tile([np.maximum(most(Z[i], snd1, src1, r, C1), np.float32(0)) * np.float32(0.05) for i in range(4)])
        U.append(mx_ref.matmul(mx_ref.quantize(w2[r]), mx_ref.quantize(h)))
    return {"y": np.stack([most(U, snd2, src2, r, C2) for r in range(N)])}

from concourse.bass import DstId, RemoteDMATransfer
from concourse.mybir import dt, AluOpType, ActivationFunctionType

N, NT, TG, C1, C2 = 8, 256, 128, 160, 32
WP = NT + N * C1
UP = NT + N * C2
BIG = 1e29

SCRATCH = {
    "xt": ("sbuf", [128, 4 * NT], "bfloat16"),
    "w1t": ("sbuf", [128, 2048], "bfloat16"),
    "w2t": ("sbuf", [128, 512], "bfloat16"),
    "ls1": ("sbuf", [128, 80], "int32"),
    "lr1": ("sbuf", [128, 64], "int32"),
    "ls2": ("sbuf", [128, 16], "int32"),
    "lr2": ("sbuf", [128, 32], "int32"),
    "of0": ("sbuf", [128, 80], "uint16"),
    "of1": ("sbuf", [128, 80], "uint16"),
    "of2": ("sbuf", [128, 80], "uint16"),
    "of3": ("sbuf", [128, 80], "uint16"),
    "or1": ("sbuf", [128, 64], "uint16"),
    "ti2": ("sbuf", [128, 16], "int32"),
    "os2": ("sbuf", [128, 14], "uint16"),
    "or2": ("sbuf", [128, 32], "uint16"),
    "xg": ("sbuf", [128, 7 * 4 * C1], "bfloat16"),
    "xgq": ("sbuf", [128, 7 * C1], "float8_e4m3fn_x4"),
    "xgs": ("sbuf", [128, 7 * C1], "uint8"),
    "xq": ("sbuf", [128, NT], "float8_e4m3fn_x4"),
    "xs": ("sbuf", [128, NT], "uint8"),
    "w1q": ("sbuf", [128, 512], "float8_e4m3fn_x4"),
    "w1s": ("sbuf", [128, 512], "uint8"),
    "w2q": ("sbuf", [128, 128], "float8_e4m3fn_x4"),
    "w2s": ("sbuf", [128, 128], "uint8"),
    "aq1": ("sbuf", [128, 7 * C1], "float8_e4m3fn_x4"),
    "as1": ("sbuf", [128, 7 * C1], "uint8"),
    "aq2": ("sbuf", [128, 7 * C2], "float8_e4m3fn_x4"),
    "as2": ("sbuf", [128, 7 * C2], "uint8"),
    "hq1": ("sbuf", [128, C1], "float8_e4m3fn_x4"),
    "hs1": ("sbuf", [128, C1], "uint8"),
    "hq2": ("sbuf", [128, 2 * C2], "float8_e4m3fn_x4"),
    "hs2": ("sbuf", [128, 2 * C2], "uint8"),
    "wz": ("sbuf", [128, 4 * WP], "bfloat16"),
    "gt": ("sbuf", [128, 4 * 4 * NT], "bfloat16"),
    "sc": ("sbuf", [128, 4 * 4 * NT], "bfloat16"),
    "m1": ("sbuf", [128, 4 * NT], "bfloat16"),
    "m2": ("sbuf", [128, 2 * TG], "float32"),
    "hg": ("sbuf", [128, 4 * 256], "bfloat16"),
    "hgq": ("sbuf", [128, 256], "float8_e4m3fn_x4"),
    "hgs": ("sbuf", [128, 256], "uint8"),
    "ht": ("sbuf", [128, 4 * NT], "bfloat16"),
    "htq": ("sbuf", [128, NT], "float8_e4m3fn_x4"),
    "hts": ("sbuf", [128, NT], "uint8"),
    "uz": ("sbuf", [128, UP], "float32"),
    "gu": ("sbuf", [128, 4 * TG], "float32"),
    "su": ("sbuf", [128, 4 * TG], "float32"),
    "yt": ("sbuf", [128, TG], "float32"),
    "ps": ("psum", [128, 4096], "float32"),
}
SEMAPHORES = (["dx", "dw1", "dw2", "ds1", "dr1", "ds2", "dr2", "mz", "mk", "ml", "xo", "w1r", "w2r", "cr1", "ct2", "cs2", "cr2",
               "sgr", "sgd", "hqr", "hqd", "hc", "hor", "m2o", "m2a", "m2b", "ud", "g2a", "g2b", "sca", "yc", "ys",
               "sent", "rc1", "rs1", "rc2", "rs2", "gh0", "gh1", "gh2", "gh3a", "gh3b", "sc0", "sc1", "sc2", "sc3"]
              + ["of%d" % t for t in range(4)] + ["xg%d" % c for c in range(4)] + ["xq%d" % c for c in range(4)]
              + ["mm%d_%d" % (k, i) for k in range(8) for i in range(4)] + ["fr%d" % k for k in range(8)]
              + ["arr%d_%d" % (l, s) for l in (1, 2) for s in range(N)])

CHUNKS = ((0, 1), (2, 3), (4,), (5, 6))
SCALAR = (((0, 0), (0, 1), (1, 0), (1, 1)), ((0, 0), (0, 1), (1, 0), (1, 1), (1, 2)), ((0, 0), (0, 1)),
          ((0, 0), (0, 1), (1, 0), (1, 1), (1, 2)))


def plan(s, T, topo):
    me = T.cores[s]
    near = [r for r in range(N) if r == s or topo.may_write(me, T.cores[r])]
    far = [r for r in range(N) if r not in near]
    i = near.index(s)
    relayed = [far[(i + k) % len(far)] for k in range(len(far))]
    direct = [near[(i + k) % len(near)] for k in range(1, len(near))]
    help_ = [c for c in topo.cores_of(me) if c != me and all(topo.may_write(c, T.cores[r]) for r in far)]
    other = [c for c in help_ if topo.die(c) != topo.die(me)]
    own = [c for c in help_ if topo.die(c) == topo.die(me)]
    return relayed, direct, (other + own)[:4], own[:2]


def bits(es):
    return sum(1 << e for e in es)


def place(s, r):
    return s if s < r else s - 1


DC2 = (slice(0, 4), slice(4, 6), slice(6, 8))
DS2 = (slice(0, 2), slice(2, 4), slice(4, 8))


def landed(layer, s, r, T, topo):
    relayed, direct, _, _ = plan(s, T, topo)
    if layer == 1:
        return 16 if r in relayed or r == direct[0] else 8
    if r in relayed:
        return 8
    j = direct.index(r)
    return DC2[j].stop - DC2[j].start + DS2[j].stop - DS2[j].start


def b8(v):
    return v.bitcast(dt.uint8)


def rank_program(g, core, T, topo):
    rank = T.rank_of(core)
    S = T.sem
    if rank is None:
        for c in topo.cores_of(core):
            s = T.rank_of(c)
            if s is not None:
                helper(g, core, s, T, topo)
        return
    relayed, direct, help1, help2 = plan(rank, T, topo)
    order = relayed + direct
    V, P, A, Y = g.vector, g.tensor, g.scalar, g.sync
    mult, add, mx = AluOpType.mult, AluOpType.add, AluOpType.max
    COPY, RELU = ActivationFunctionType.Copy, ActivationFunctionType.Relu

    Y.dma_start(T.xt[:], T.x[:]).then_inc(S.dx, 16)
    for q in range(8):
        (Y if q < 3 else A).dma_start(T.ls1[16 * q:16 * q + 16, :], T.snd1[:, :]).then_inc(S.ds1, 16)
    Y.dma_start(T.w1t[:], T.w1[:]).then_inc(S.dw1, 16)
    for dst, src, sem in ((T.lr1, T.src1, S.dr1), (T.ls2, T.snd2, S.ds2)):
        for q in range(8):
            Y.dma_start(dst[16 * q:16 * q + 16, :], src[:, :]).then_inc(sem, 16)
    Y.dma_start(T.w2t[:], T.w2[:]).then_inc(S.dw2, 16)
    for q in range(8):
        Y.dma_start(T.lr2[16 * q:16 * q + 16, :], T.src2[:, :]).then_inc(S.dr2, 16)

    for t in range(4):
        a = t * WP + NT + rank * C1
        V.memset(T.wz[:, a:a + C1], 0.0).then_inc(S.mz, 1)
    V.memset(T.uz[:, NT + rank * C2:NT + rank * C2 + C2], 0.0).then_inc(S.mz, 1)
    V.memset(T.hg[:, 4 * 7 * C2:1024], 0.0).then_inc(S.mz, 1)
    V.memset(T.m1[:], 1.0).then_inc(S.mk, 1)
    V.memset(T.m2[:], BIG).then_inc(S.mk, 1)
    V.wait_ge(S.mk, 2)
    V.memset(T.m1[:, 0:4 * NT:4], 0.0).then_inc(S.ml, 1)
    V.memset(T.m2[:, 0:2 * TG:4], -BIG).then_inc(S.ml, 1)

    V.wait_ge(S.ds1, 128)
    V.tensor_scalar(T.of0[:], T.ls1[:], 4, 0, mult, mx).then_inc(S.of0, 1)
    V.wait_ge(S.of0, 1)
    for t in (1, 2, 3):
        V.tensor_scalar(T["of%d" % t][:], T.of0[:], t, None, add).then_inc(S["of%d" % t], 1)

    def pick(eng, pos, t, sem):
        r = order[pos]
        out = T.xg[:, 4 * C1 * pos + t:4 * C1 * (pos + 1):4]
        win = T.xt[:, :].indirect(T["of%d" % t][:, 10 * r:10 * r + 10])
        if eng is V:
            V.tensor_copy(out, win).then_inc(sem, 1)
        else:
            A.activation(out, win, COPY).then_inc(sem, 1)

    A.wait_ge(S.dx, 16)
    A.wait_ge(S.of0, 1)
    A.wait_ge(S.of1, 1)
    V.wait_ge(S.dx, 16)
    for t in (1, 2, 3):
        V.wait_ge(S["of%d" % t], 1)
    for c, chunk in enumerate(CHUNKS):
        sem = S["xg%d" % c]
        if c == 1:
            A.wait_ge(S.of2, 1)
        for j, t in SCALAR[c]:
            pick(A, chunk[j], t, sem)
        for j in range(len(chunk)):
            for t in range(4):
                if (j, t) not in SCALAR[c]:
                    pick(V, chunk[j], t, sem)
        V.wait_ge(sem, 4 * len(chunk))
        a, b = C1 * chunk[0], C1 * (chunk[-1] + 1)
        V.quantize_mx(T.xgq[:, a:b], T.xgs[:, a:b], T.xg[:, 4 * a:4 * b]).then_inc(S["xq%d" % c], 1)

    V.quantize_mx(T.xq[:], T.xs[:], T.xt[:]).then_inc(S.xo, 1)
    V.wait_ge(S.dw1, 16)
    V.quantize_mx(T.w1q[:], T.w1s[:], T.w1t[:]).then_inc(S.w1r, 1)
    V.wait_ge(S.dr1, 128)
    V.tensor_copy(T.or1[:], T.lr1[:]).then_inc(S.cr1, 1)
    V.wait_ge(S.ds2, 128)
    V.tensor_scalar(T.ti2[:], T.ls2[:], 4, 3, mult, add).then_inc(S.ct2, 1)
    V.wait_ge(S.ct2, 1)
    for pos, r in enumerate(order):
        V.tensor_scalar(T.os2[:, 2 * pos:2 * pos + 2], T.ti2[:, 2 * r:2 * r + 2], 0, None, mx).then_inc(S.cs2, 1)
    V.wait_ge(S.dw2, 16)
    V.quantize_mx(T.w2q[:], T.w2s[:], T.w2t[:]).then_inc(S.w2r, 1)
    V.wait_ge(S.dr2, 128)
    V.tensor_copy(T.or2[:], T.lr2[:]).then_inc(S.cr2, 1)

    def rankof(way, p):
        for s in range(N):
            if s != rank:
                rl, di, _, _ = plan(s, T, topo)
                if (rl if way == "r" else di)[p] == rank:
                    return s

    srcs = [rankof(w, p) for w, p in (("r", 0), ("r", 1), ("d", 0), ("r", 2), ("r", 3), ("d", 1), ("d", 2))]
    P.wait_ge(S.w1r, 1)
    for k in range(8):
        if k == 0:
            P.wait_ge(S.xo, 1)
            n, base, mq, ms = NT, 0, T.xq[:], T.xs[:]
        else:
            s = srcs[k - 1]
            P.wait_ge(S["arr1_%d" % s], landed(1, s, rank, T, topo))
            a = C1 * place(s, rank)
            n, base, mq, ms = C1, NT + C1 * s, T.aq1[:, a:a + C1], T.as1[:, a:a + C1]
        if k >= 2:
            P.wait_ge(S["fr%d" % (k - 2)], 4)
        for i in (0, 2, 1, 3):
            bank = 512 * (4 * (k % 2) + i)
            done = S["mm%d_%d" % (k, i)]
            P.matmul_mx(T.ps[:, bank:bank + n], T.w1q[:, 128 * i:128 * i + 128], T.w1s[:, 128 * i:128 * i + 128],
                        mq, ms, True, True).then_inc(done, 1)
            out, res = T.wz[:, WP * i + base:WP * i + base + n], T.ps[:, bank:bank + n]
            if i < 2:
                V.wait_ge(done, 1)
                V.tensor_scalar(out, res, 0.05, 0.0, mult, mx).then_inc(S["fr%d" % k], 1)
            else:
                A.wait_ge(done, 1)
                A.activation(out, res, RELU, scale=0.05).then_inc(S["fr%d" % k], 1)

    for e in (V, A):
        e.wait_ge(S.mz, 6)
        e.wait_ge(S.cr1, 1)
        e.wait_ge(S.fr6, 4)
        e.wait_ge(S.fr7, 4)
    V.wait_ge(S.ml, 2)
    V.wait_ge(S.cs2, 7)

    def sources(eng, t, h, sem):
        out = T.gt[:, 1024 * t + 512 * h:1024 * t + 512 * h + 512]
        win = T.wz[:, WP * t:WP * (t + 1)].indirect(T.or1[:, 32 * h:32 * h + 32])
        if eng is V:
            V.tensor_copy(out, win).then_inc(sem, 1)
        else:
            A.activation(out, win, COPY).then_inc(sem, 1)

    def scan(t, a, b):
        o = 1024 * t
        V.tensor_tensor_scan(T.sc[:, o + a:o + b], T.m1[:, a:b], T.gt[:, o + a:o + b], 0.0, mult, mx).then_inc(S["sc%d" % t], 1)

    def chosen(t, a, b, sem):
        V.tensor_copy(T.hg[:, 4 * a + t:4 * b:4],
                      T.sc[:, 1024 * t:1024 * t + 1024].indirect(T.os2[:, a // 16:b // 16])).then_inc(sem, 1)

    sources(A, 0, 0, S.gh0)
    sources(A, 1, 0, S.gh1)
    sources(A, 2, 0, S.gh2)
    sources(A, 2, 1, S.gh2)
    sources(A, 3, 0, S.gh3a)
    sources(A, 3, 1, S.gh3b)

    sources(V, 0, 1, S.gh0)
    V.wait_ge(S.gh0, 2)
    scan(0, 0, 1024)
    sources(V, 1, 1, S.gh1)
    V.wait_ge(S.gh1, 2)
    scan(1, 0, 1024)
    V.wait_ge(S.sc0, 1)
    chosen(0, 0, 7 * C2, S.sgr)
    V.wait_ge(S.sc1, 1)
    chosen(1, 0, 7 * C2, S.sgr)
    V.wait_ge(S.gh2, 2)
    scan(2, 0, 1024)
    V.wait_ge(S.sc2, 1)
    chosen(2, 0, 7 * C2, S.sgr)
    V.wait_ge(S.gh3a, 1)
    scan(3, 0, 512)
    V.wait_ge(S.gh3b, 1)
    scan(3, 512, 1024)
    V.wait_ge(S.sc3, 2)
    chosen(3, 0, 128, S.sgr)
    V.wait_ge(S.sgr, 4)
    V.quantize_mx(T.hgq[:, 0:128], T.hgs[:, 0:128], T.hg[:, 0:512]).then_inc(S.hqr, 1)
    chosen(3, 128, 7 * C2, S.sgd)
    V.wait_ge(S.sgd, 1)
    V.quantize_mx(T.hgq[:, 128:256], T.hgs[:, 128:256], T.hg[:, 512:1024]).then_inc(S.hqd, 1)

    for t in range(4):
        A.wait_ge(S["sc%d" % t], 2 if t == 3 else 1)
        A.activation(T.ht[:, t:4 * NT:4], T.sc[:, 1024 * t + 3:1024 * t + 1024:4], COPY).then_inc(S.hc, 1)
    V.wait_ge(S.hc, 4)
    V.quantize_mx(T.htq[:], T.hts[:], T.ht[:]).then_inc(S.hor, 1)

    P.wait_ge(S.w2r, 1)
    P.wait_ge(S.hor, 1)
    P.matmul_mx(T.ps[:, 0:NT], T.w2q[:], T.w2s[:], T.htq[:], T.hts[:], True, True).then_inc(S.m2o, 1)
    V.wait_ge(S.m2o, 1)
    V.tensor_copy(T.uz[:, 0:NT], T.ps[:, 0:NT]).then_inc(S.ud, 1)
    for s in range(N):
        if s != rank:
            P.wait_ge(S["arr2_%d" % s], landed(2, s, rank, T, topo))
    P.matmul_mx(T.ps[:, 2048:2176], T.w2q[:], T.w2s[:], T.aq2[:, 0:128], T.as2[:, 0:128], True, True).then_inc(S.m2a, 1)
    P.matmul_mx(T.ps[:, 2560:2688], T.w2q[:], T.w2s[:], T.aq2[:, 96:224], T.as2[:, 96:224], True, True).then_inc(S.m2b, 1)
    V.wait_ge(S.m2a, 1)
    A.wait_ge(S.m2b, 1)
    done, hole = 1, C2 * rank
    for a, b, bank in ((0, 112, 2048), (112, 224, 2560 - 96)):
        for lo, hi in ((a, min(b, hole)), (max(a, hole), b)):
            if lo < hi:
                o = NT + lo + (C2 if lo >= hole else 0)
                out, res = T.uz[:, o:o + hi - lo], T.ps[:, bank + lo:bank + hi]
                if a == 0:
                    V.tensor_copy(out, res).then_inc(S.ud, 1)
                else:
                    A.activation(out, res, COPY).then_inc(S.ud, 1)
                done += 1

    V.wait_ge(S.cr2, 1)
    A.wait_ge(S.cr2, 1)
    V.wait_ge(S.ud, done)
    A.wait_ge(S.ud, done)
    V.tensor_copy(T.gu[:, 0:256], T.uz[:, :].indirect(T.or2[:, 0:16])).then_inc(S.g2a, 1)
    A.activation(T.gu[:, 256:512], T.uz[:, :].indirect(T.or2[:, 16:32]), COPY).then_inc(S.g2b, 1)
    for h, sem in ((0, S.g2a), (256, S.g2b)):
        V.wait_ge(sem, 1)
        V.tensor_tensor_scan(T.su[:, h:h + 256], T.m2[:], T.gu[:, h:h + 256], 0.0, AluOpType.min, mx).then_inc(S.sca, 1)
    V.wait_ge(S.sca, 2)
    V.tensor_copy(T.yt[:], T.su[:, 3:4 * TG:4]).then_inc(S.yc, 1)
    Y.wait_ge(S.yc, 1)
    Y.dma_start(T.y[:], T.yt[:]).then_inc(S.ys, 16)
    Y.wait_ge(S.ys, 16)

    sent = [0]

    def fused(parts):
        ts = []
        for d, es, src, dst, sem in parts:
            rid, pid = topo.addr(d, core)
            ts.append(RemoteDMATransfer(dst_ids=[DstId(rid=rid, pnc=pid)], dma_engine_mask=bits(es), remote_sem=sem,
                                        src=src, dst=dst))
            sent[0] += len(es)
        g.remote_dma_fused(ts, local_sem=S.sent)

    for c, chunk in enumerate(CHUNKS):
        g.wait_ge(S["xq%d" % c], 1)
        codes, planes = [], []
        for j, pos in enumerate(chunk):
            a = C1 * pos
            r = order[pos]
            d = help1[pos] if pos < 4 else T.cores[r]
            es = topo.engines(core, d)
            w = len(es) // len(chunk)
            es = es[w * j:w * j + w]
            sq, ss = b8(T.xgq[:, a:a + C1]), T.xgs[:, a:a + C1]
            if pos < 4:
                codes.append((d, es, sq, b8(T.hq1[:, :]), S.rc1))
                planes.append((d, es, ss, T.hs1[:, :], S.rs1))
            else:
                o = C1 * place(rank, r)
                sem = S["arr1_%d" % rank]
                codes.append((d, es, sq, b8(T.aq1[:, o:o + C1]), sem))
                planes.append((d, es, ss, T.as1[:, o:o + C1], sem))
        fused(codes)
        fused(planes)

    g.wait_ge(S.hqr, 1)
    codes, planes = [], []
    for j, d in enumerate(help2):
        es = topo.engines(core, d)
        es = es[len(es) // 2 * j:len(es) // 2 * (j + 1)]
        a = 2 * C2 * j
        codes.append((d, es, b8(T.hgq[:, a:a + 2 * C2]), b8(T.hq2[:, :]), S.rc2))
        planes.append((d, es, T.hgs[:, a:a + 2 * C2], T.hs2[:, :], S.rs2))
    fused(codes)
    fused(planes)
    g.wait_ge(S.hqd, 1)
    codes, planes = [], []
    for j, r in enumerate(direct):
        d = T.cores[r]
        es = topo.engines(core, d)
        a, o = C2 * (4 + j), C2 * place(rank, r)
        sem = S["arr2_%d" % rank]
        codes.append((d, es[DC2[j]], b8(T.hgq[:, a:a + C2]), b8(T.aq2[:, o:o + C2]), sem))
        planes.append((d, es[DS2[j]], T.hgs[:, a:a + C2], T.as2[:, o:o + C2], sem))
    fused(codes)
    fused(planes)
    g.wait_ge(S.sent, sent[0])


def helper(g, core, s, T, topo):
    relayed, _, help1, help2 = plan(s, T, topo)
    S = T.sem
    me = T.cores[s]
    sent = 0
    if core in help1:
        j = help1.index(core)
        w = len(topo.engines(me, core)) // 2
        r = relayed[j]
        d = T.cores[r]
        o = C1 * place(s, r)
        rid, pid = topo.addr(d, core)
        for sem, out, src in ((S.rc1, b8(T.aq1[:, o:o + C1]), b8(T.hq1[:, :])), (S.rs1, T.as1[:, o:o + C1], T.hs1[:, :])):
            g.wait_ge(sem, w)
            g.remote_dma(out, src, S["arr1_%d" % s], S.sent, pid, rid, topo.mask(core, d))
            sent += len(topo.engines(core, d))
    if core in help2:
        j = help2.index(core)
        w = len(topo.engines(me, core)) // 2
        two = relayed[2 * j:2 * j + 2]
        for sem, code in ((S.rc2, True), (S.rs2, False)):
            g.wait_ge(sem, w)
            ts = []
            for i, r in enumerate(two):
                d = T.cores[r]
                es = topo.engines(core, d)[4 * i:4 * i + 4]
                o, a = C2 * place(s, r), C2 * i
                src = b8(T.hq2[:, a:a + C2]) if code else T.hs2[:, a:a + C2]
                dst = b8(T.aq2[:, o:o + C2]) if code else T.as2[:, o:o + C2]
                rid, pid = topo.addr(d, core)
                ts.append(RemoteDMATransfer(dst_ids=[DstId(rid=rid, pnc=pid)], dma_engine_mask=bits(es),
                                            remote_sem=S["arr2_%d" % s], src=src, dst=dst))
                sent += len(es)
            g.remote_dma_fused(ts, local_sem=S.sent)
    if sent:
        g.wait_ge(S.sent, sent)
